import numpy as np
import ml_dtypes


def mxq(x, axis, fmt="e4m3"):
    dtype, down = {"e4m3": (ml_dtypes.float8_e4m3fn, 7), "e5m2": (ml_dtypes.float8_e5m2, 14)}[fmt]
    v = np.moveaxis(np.asarray(x, np.float32).astype(ml_dtypes.bfloat16).astype(np.float64), axis, -1)
    blocks = v.reshape(v.shape[:-1] + (-1, 32))
    amax = np.abs(blocks).max(-1, keepdims=True)
    byte = np.maximum(np.where(amax > 0, np.frexp(amax)[1] - 1 + 127, 0) - down, 1)
    scale = np.exp2(byte - 127.0)
    codes = (blocks / scale).astype(np.float32).astype(dtype).astype(np.float64)
    return np.moveaxis((codes * scale).reshape(v.shape), -1, axis)


WIDE = False


def mx_kscale(k):
    if not WIDE:
        return np.ones(k)
    levels = np.array([18, -18])
    if k % 512:
        return np.exp2(np.random.permutation(np.resize(levels, k // 32))).repeat(32)
    a = np.empty((k // 512, 16))
    for p in range(k // 512):
        a[p, :8] = np.random.permutation(np.resize(levels, 8))
        for g in range(8):
            far = levels[np.abs(levels - a[p, g]) >= 10]
            a[p, g + 8] = far[np.random.randint(len(far))]
    return np.exp2(a.ravel()).repeat(32)


def f64(x):
    return np.asarray(x).astype(np.float64)


def striped(idx):
    return np.tile(np.asarray(idx).reshape(-1, 16).T, (8, 1)).astype(np.uint16)


def unstriped(offs):
    return offs[:16].T.reshape(-1).astype(np.int64)


def sig(x):
    return 1.0 / (1.0 + np.exp(-x))


def setup_inputs():
    n = np.random.standard_normal
    uni = np.random.uniform
    idx = np.random.permutation(2048)[:512]
    f_d = mx_kscale(512)
    f_e = mx_kscale(512)
    f_r = mx_kscale(512)
    return {
        "xT": (n((512, 512)) * f_d[:, None] * f_r[None, :]).astype(np.float32),
        "wg": (n((512, 2048)) / np.sqrt(512) / f_d[:, None]).astype(np.float32),
        "wu": (n((512, 2048)) / np.sqrt(512) / f_d[:, None]).astype(np.float32),
        "dyT": (n((512, 512)) * f_e[:, None]).astype(np.float32),
        "wd": (n((512, 2048)) / np.sqrt(512) / f_e[:, None]).astype(np.float32),
        "us": (uni(0.75, 1.3, (512, 1)) / f_r[:, None]).astype(np.float32),
        "tg": np.tile(uni(0.75, 1.3, 2048), (128, 1)).astype(np.float32),
        "tu": np.tile(uni(0.75, 1.3, 2048), (128, 1)).astype(np.float32),
        "wt": (uni(0.75, 1.3, (512, 1)) / np.sqrt(512)).astype(np.float32),
        "offs": striped(idx),
    }


def reference(xT, wg, wu, dyT, wd, us, tg, tu, wt, offs):
    idx = unstriped(offs)
    wg_i = f64(wg)[:, idx]
    wu_i = f64(wu)[:, idx]
    wd_i = f64(wd)[:, idx]
    tg_i = f64(tg)[:1][:, idx]
    tu_i = f64(tu)[:1][:, idx]
    q_xT = mxq(f64(xT), 0, "e4m3")
    ag = q_xT.T @ mxq(wg_i, 0, "e4m3")
    au = q_xT.T @ mxq(wu_i, 0, "e4m3")
    z = f64(us) * tg_i * ag
    b = f64(us) * tu_i * au
    dh = mxq(f64(dyT), 0, "e5m2").T @ mxq(wd_i, 0, "e4m3")
    s = sig(z)
    dg = f64(wt) * f64(us) * tg_i * dh * b * s * (1.0 + z * (1.0 - s))
    du = f64(wt) * f64(us) * tu_i * dh * z * s
    q_xT_2 = mxq(f64(xT), 1, "e4m3")
    dwg = q_xT_2 @ mxq(dg, 0, "e5m2")
    dwu = q_xT_2 @ mxq(du, 0, "e5m2")
    out_0 = np.zeros((512, 2048))
    out_0[:, idx] = dwg
    out_1 = np.zeros((512, 2048))
    out_1[:, idx] = dwu
    return out_0, out_1

@@ -1,0 +1,255 @@
+from contextlib import ExitStack
+
+import concourse.mybir as mybir
+from concourse.masks import make_identity
+
+D, R, SLOTS, UNITS = 512, 512, 512, 2048
+FLOPS = 5 * 2 * 512 * 512 * 512
+
+F32 = mybir.dt.float32
+BF16 = mybir.dt.bfloat16
+U32 = mybir.dt.uint32
+U16 = mybir.dt.uint16
+U8 = mybir.dt.uint8
+E4M3 = mybir.dt.float8_e4m3fn_x4
+E5M2 = mybir.dt.float8_e5m2_x4
+ALU = mybir.AluOpType
+ACT = mybir.ActivationFunctionType
+
+P = 128
+PACK = 4
+BLOCKS = 4
+WINDOWS = 3
+
+
+def block(b):
+    return slice(b * P, (b + 1) * P)
+
+
+def tile_attend_gglu_w_kernel(tc, xT, wg, wu, dyT, wd, us, tg, tu, wt, offs, out_0, out_1):
+    nc = tc.nc
+    with ExitStack() as ctx:
+        keep = ctx.enter_context(tc.tile_pool(name="keep", bufs=1))
+        psum = ctx.enter_context(tc.psum_pool(name="psum", bufs=1))
+
+        def sb(name, cols, dtype, tag=None):
+            return keep.tile([P, cols], dtype, name=name, tag=tag or name, align_bytes=64)
+
+        def mx_operand(name, fmt):
+            return sb(name + "_codes", 512, U32), sb(name + "_scales", 512, U8), fmt
+
+        def quantize(operand, src, cols=slice(0, 512)):
+            codes, scales, fmt = operand
+            nc.vector.quantize_mx(out=codes[:, cols].bitcast(fmt), scales=scales[:, cols], in_=src)
+
+        def product(bank, stationary, b, moving):
+            nc.tensor.matmul_mx(
+                out=bank[:],
+                lhsT=stationary[0][:, block(b)].bitcast(stationary[2]),
+                lhsT_scale=stationary[1][:, block(b)],
+                rhs=moving[0][:].bitcast(moving[2]),
+                rhs_scale=moving[1][:],
+                start=True,
+                stop=True,
+            )
+
+        def weave(engine_copy, dst, planes):
+            engine_copy(
+                out=dst.rearrange("p (c i t) -> p c t i", i=4, t=PACK),
+                in_=planes.rearrange("p t (c i) -> p c t i", i=4),
+            )
+
+        banks = [psum.tile([P, 512], F32, name="bank%d" % b) for b in range(8)]
+        low, high = banks[:4], banks[4:]
+
+        offsets = keep.tile([P, SLOTS // 16], U16, name="offsets")
+        nc.sync.dma_start(offsets[:], offs)
+
+        us_col = sb("us_col", BLOCKS, F32)
+        wt_col = sb("wt_col", BLOCKS, F32)
+        with nc.allow_non_contiguous_dma(reason="one number a row, onto the partitions"):
+            nc.scalar.dma_start(out=us_col[:], in_=us.rearrange("(m c) o -> c (m o)", c=P))
+            nc.scalar.dma_start(out=wt_col[:], in_=wt.rearrange("(m c) o -> c (m o)", c=P))
+        x_raw = keep.tile([P, PACK, R], F32, name="x_raw")
+        dy_raw = keep.tile([P, PACK, R], F32, name="dy_raw")
+
+        def plane_tiles(name, tag):
+            return [sb("%s%d" % (name, t), UNITS, F32, "%s%d" % (tag, t)) for t in range(PACK)]
+
+        def load_plane(planes, matrix, t):
+            nc.sync.dma_start(out=planes[t][:], in_=matrix.rearrange("(p t) c -> p t c", t=PACK)[:, t, :])
+
+        def load_planes(name, matrix, tag):
+            planes = plane_tiles(name, tag)
+            for t in range(PACK):
+                load_plane(planes, matrix, t)
+            return planes
+
+        wg_planes = plane_tiles("wg", "first")
+        for q in range(4):
+            cols = slice(512 * q, 512 * (q + 1))
+            nc.sync.dma_start(out=wg_planes[0][:, cols], in_=wg.rearrange("(p t) c -> p t c", t=PACK)[:, 0, cols])
+        load_plane(wg_planes, wg, 1)
+        tg_row = sb("tg_row", UNITS, F32, "row0")
+        tu_row = sb("tu_row", UNITS, F32, "row1")
+        for row, src in ((tg_row, tg), (tu_row, tu)):
+            nc.vector.memset(row[:], 0.0)
+            nc.sync.dma_start(out=row[0:1, :], in_=src[0:1, :])
+        for t in range(2, PACK):
+            load_plane(wg_planes, wg, t)
+        nc.sync.dma_start(out=x_raw[:], in_=xT.rearrange("(p t) r -> p t r", t=PACK))
+        wd_planes = load_planes("wd", wd, "second")
+        nc.sync.dma_start(out=dy_raw[:], in_=dyT.rearrange("(p t) r -> p t r", t=PACK))
+
+        ident = sb("ident", P, F32)
+        make_identity(nc, ident[:])
+
+        windows_1 = [sb("window_1_%d" % w, UNITS, F32) for w in range(2)]
+        for window in windows_1:
+            nc.vector.memset(window[:], 0.0)
+
+        staged = [sb("staged%d" % m, 512, F32) for m in range(BLOCKS)]
+        for n, row in enumerate((tg_row, tu_row)):
+            nc.vector.tensor_copy(staged[n][:], row[:].indirect(offsets[:]))
+            for j in range(BLOCKS):
+                nc.tensor.transpose(high[n][:, block(j)], staged[n][:, block(j)], ident[:])
+        tg_col = sb("tg_col", BLOCKS, F32)
+        tg_neg_half = sb("tg_neg_half", BLOCKS, F32)
+        tu_col = sb("tu_col", BLOCKS, F32)
+        tg_tu = sb("tg_tu", BLOCKS, F32)
+        nc.scalar.copy(out=tg_col[:], in_=high[0][:, 0:512:P])
+        nc.scalar.mul(tg_neg_half[:], high[0][:, 0:512:P], -0.5)
+        nc.scalar.copy(out=tu_col[:], in_=high[1][:, 0:512:P])
+        nc.vector.tensor_tensor(tg_tu[:], tg_col[:], tu_col[:], ALU.mult)
+        wt_us = sb("wt_us", BLOCKS, F32)
+        wt_us_us = sb("wt_us_us", BLOCKS, F32)
+        nc.vector.tensor_tensor(wt_us[:], wt_col[:], us_col[:], ALU.mult)
+        nc.vector.tensor_tensor(wt_us_us[:], wt_us[:], us_col[:], ALU.mult)
+
+        windows_0 = [sb("window_0_0", UNITS, F32, "row0"), sb("window_0_1", UNITS, F32, "row1")]
+        for window in windows_0:
+            nc.gpsimd.memset(window[:], 0.0)
+
+        def turn(src, bank, dst):
+            words = src.bitcast(F32)
+            for u in range(2):
+                nc.tensor.transpose(bank[:, block(u)], words[:, u:256:2], ident[:])
+            nc.scalar.copy(
+                out=dst.rearrange("p (c u) -> p c u", u=2),
+                in_=bank[:, 0:256].rearrange("p (u c) -> p c u", u=2),
+            )
+
+        def turned(tile, j):
+            return tile[:, 256 * j : 256 * (j + 1)]
+
+        def gather(name, planes):
+            gathered = keep.tile([P, PACK, SLOTS], BF16, name=name)
+            for t in range(PACK):
+                nc.vector.tensor_copy(gathered[:, t, :], planes[t][:].indirect(offsets[:]))
+            return gathered
+
+        def scale_and_turn(src_banks, scale, through, dst_banks):
+            for m in range(BLOCKS):
+                nc.scalar.activation(through[m], src_banks[m][:], ACT.Copy, scale=scale[:, m : m + 1])
+                for j in range(BLOCKS):
+                    nc.tensor.transpose(dst_banks[j][:, block(m)], through[m][:, block(j)], ident[:])
+
+        wg_gathered = gather("wg_gathered", wg_planes)
+        wg_woven = sb("wg_woven", 2048, BF16)
+        weave(nc.scalar.copy, wg_woven[:], wg_gathered[:])
+        x_woven = sb("x_woven", 2048, BF16)
+        weave(nc.vector.tensor_copy, x_woven[:], x_raw[:])
+        x_d = mx_operand("x_d", E4M3)
+        quantize(x_d, x_woven[:])
+        wg_q = mx_operand("wg_q", E4M3)
+        quantize(wg_q, wg_woven[:])
+        wu_planes = load_planes("wu", wu, "first")
+        for m in range(BLOCKS):
+            product(low[m], x_d, m, wg_q)
+        scale_and_turn(low, us_col, [s[:] for s in staged], high)
+        silu = [sb("silu%d" % j, 512, F32) for j in range(BLOCKS)]
+        slope = [sb("slope%d" % j, 512, F32) for j in range(BLOCKS)]
+        for j in range(BLOCKS):
+            nc.scalar.activation(silu[j][:], high[j][:], ACT.Silu, scale=tg_col[:, j : j + 1])
+        for j in range(BLOCKS):
+            nc.scalar.activation(slope[j][:], high[j][:], ACT.Tanh, scale=tg_neg_half[:, j : j + 1])
+            nc.gpsimd.tensor_scalar(slope[j][:], slope[j][:], 0.5, 0.5, ALU.mult, ALU.add)
+
+        halves = [sb("half%d" % j, 512, BF16) for j in range(BLOCKS)]
+        x_turned = sb("x_turned", 1024, F32)
+        for t in range(PACK):
+            nc.scalar.copy(out=halves[t][:], in_=x_raw[:, t, :])
+            turn(halves[t][:], low[t], turned(x_turned, t))
+        x_r = mx_operand("x_r", E4M3)
+        quantize(x_r, x_turned[:].bitcast(BF16))
+
+        wd_gathered = gather("wd_gathered", wd_planes)
+        windows_0.append(sb("window_0_2", UNITS, F32, "second0"))
+        nc.gpsimd.memset(windows_0[2][:], 0.0)
+        wd_woven = sb("wd_woven", 2048, BF16)
+        weave(nc.scalar.copy, wd_woven[:, 0:1024], wd_gathered[:, :, 0:256])
+        weave(nc.vector.tensor_copy, wd_woven[:, 1024:2048], wd_gathered[:, :, 256:512])
+        wd_q = mx_operand("wd_q", E4M3)
+        quantize(wd_q, wd_woven[:])
+        dy_woven = sb("dy_woven", 2048, BF16)
+        dy_q = mx_operand("dy_q", E5M2)
+        for m in range(BLOCKS):
+            copy = nc.scalar.copy if m == BLOCKS - 1 else nc.vector.tensor_copy
+            weave(copy, dy_woven[:, 512 * m : 512 * (m + 1)], dy_raw[:, :, block(m)])
+        for m in range(BLOCKS):
+            quantize(dy_q, dy_woven[:, 512 * m : 512 * (m + 1)], block(m))
+            product(low[m], dy_q, m, wd_q)
+        scale_and_turn(low, wt_us, [s[:] for s in staged], high)
+
+        du_turned = sb("du_turned", 1024, F32)
+        du_q = mx_operand("du_q", E5M2)
+        for j in range(BLOCKS):
+            nc.vector.scalar_tensor_tensor(halves[j][:], high[j][:], tu_col[:, j : j + 1], silu[j][:], ALU.mult, ALU.mult)
+            turn(halves[j][:], high[j], turned(du_turned, j))
+        for j in range(BLOCKS):
+            quantize(du_q, turned(du_turned, j).bitcast(BF16), block(j))
+        for k in range(BLOCKS):
+            product(high[k], x_r, k, du_q)
+
+        for m in range(BLOCKS):
+            nc.scalar.activation(x_raw[:, m, :], low[m][:], ACT.Copy, scale=wt_us_us[:, m : m + 1])
+        for m in range(BLOCKS):
+            for j in range(BLOCKS):
+                nc.tensor.transpose(low[j][:, block(m)], x_raw[:, m, block(j)], ident[:])
+
+        wu_gathered = gather("wu_gathered", wu_planes)
+        wu_woven = sb("wu_woven", 2048, BF16)
+        weave(nc.scalar.copy, wu_woven[:], wu_gathered[:])
+
+        for j in range(BLOCKS):
+            nc.vector.scalar_tensor_tensor(slope[j][:], silu[j][:], -1.0, slope[j][:], ALU.add, ALU.mult)
+        for j in range(BLOCKS):
+            nc.vector.scalar_tensor_tensor(slope[j][:], slope[j][:], 1.0, low[j][:], ALU.add, ALU.mult)
+
+        def put(bank, through, window, out, k):
+            nc.scalar.copy(out=through, in_=bank[:])
+            nc.vector.tensor_copy(window[:].indirect(offsets[:]), through)
+            nc.sync.dma_start(out=out.rearrange("(p t) c -> p t c", t=PACK)[:, k, :], in_=window[:])
+
+        first_result = sb("first_result", 512, F32, "first3")
+        put(high[0], first_result[:], windows_1[0], out_1, 0)
+
+        wu_q = mx_operand("wu_q", E4M3)
+        quantize(wu_q, wu_woven[:])
+        put(high[1], wu_woven[:, 0:1024].bitcast(F32), windows_1[1], out_1, 1)
+
+        for j in range(BLOCKS):
+            product(low[j], wu_q, j, x_d)
+        dg_turned = sb("dg_turned", 1024, F32)
+        for j in range(BLOCKS):
+            nc.vector.scalar_tensor_tensor(halves[j][:], low[j][:], tg_tu[:, j : j + 1], slope[j][:], ALU.mult, ALU.mult)
+            turn(halves[j][:], low[j], turned(dg_turned, j))
+        put(high[2], slope[BLOCKS - 1][:], windows_1[0], out_1, 2)
+
+        dg_q = mx_operand("dg_q", E5M2)
+        quantize(dg_q, dg_turned[:].bitcast(BF16))
+        put(high[3], dg_turned[:, 0:512], windows_1[1], out_1, 3)
+
+        for k in range(BLOCKS):
+            product(low[k], x_r, k, dg_q)
+            put(low[k], staged[k][:], windows_0[k % WINDOWS], out_0, k)

@@ -20,6 +20,7 @@ P = 128
 PACK = 4
 BLOCKS = 4
 WINDOWS = 3
+SCALAR_SLOTS = 192
 
 
 def block(b):
@@ -35,8 +36,8 @@ def tile_attend_gglu_w_kernel(tc, xT, wg, wu, dyT, wd, us, tg, tu, wt, offs, out
         def sb(name, cols, dtype, tag=None):
             return keep.tile([P, cols], dtype, name=name, tag=tag or name, align_bytes=64)
 
-        def mx_operand(name, fmt):
-            return sb(name + "_codes", 512, U32), sb(name + "_scales", 512, U8), fmt
+        def mx_operand(name, fmt, tag=None):
+            return sb(name + "_codes", 512, U32, tag), sb(name + "_scales", 512, U8), fmt
 
         def quantize(operand, src, cols=slice(0, 512)):
             codes, scales, fmt = operand
@@ -68,16 +69,19 @@ def tile_attend_gglu_w_kernel(tc, xT, wg, wu, dyT, wd, us, tg, tu, wt, offs, out
         us_col = sb("us_col", BLOCKS, F32)
         wt_col = sb("wt_col", BLOCKS, F32)
         with nc.allow_non_contiguous_dma(reason="one number a row, onto the partitions"):
-            nc.scalar.dma_start(out=us_col[:], in_=us.rearrange("(m c) o -> c (m o)", c=P))
-            nc.scalar.dma_start(out=wt_col[:], in_=wt.rearrange("(m c) o -> c (m o)", c=P))
+            nc.sync.dma_start(out=us_col[:], in_=us.rearrange("(m c) o -> c (m o)", c=P))
+            nc.sync.dma_start(out=wt_col[:], in_=wt.rearrange("(m c) o -> c (m o)", c=P))
         x_raw = keep.tile([P, PACK, R], F32, name="x_raw")
         dy_raw = keep.tile([P, PACK, R], F32, name="dy_raw")
 
         def plane_tiles(name, tag):
             return [sb("%s%d" % (name, t), UNITS, F32, "%s%d" % (tag, t)) for t in range(PACK)]
 
-        def load_plane(planes, matrix, t):
-            nc.sync.dma_start(out=planes[t][:], in_=matrix.rearrange("(p t) c -> p t c", t=PACK)[:, t, :])
+        def load_plane(planes, matrix, t, pieces=1):
+            width = UNITS // pieces
+            for q in range(pieces):
+                cols = slice(width * q, width * (q + 1))
+                nc.sync.dma_start(out=planes[t][:, cols], in_=matrix.rearrange("(p t) c -> p t c", t=PACK)[:, t, cols])
 
         def load_planes(name, matrix, tag):
             planes = plane_tiles(name, tag)
@@ -85,50 +89,58 @@ def tile_attend_gglu_w_kernel(tc, xT, wg, wu, dyT, wd, us, tg, tu, wt, offs, out
                 load_plane(planes, matrix, t)
             return planes
 
-        wg_planes = plane_tiles("wg", "first")
-        for q in range(4):
-            cols = slice(512 * q, 512 * (q + 1))
-            nc.sync.dma_start(out=wg_planes[0][:, cols], in_=wg.rearrange("(p t) c -> p t c", t=PACK)[:, 0, cols])
-        load_plane(wg_planes, wg, 1)
-        tg_row = sb("tg_row", UNITS, F32, "row0")
-        tu_row = sb("tu_row", UNITS, F32, "row1")
-        for row, src in ((tg_row, tg), (tu_row, tu)):
-            nc.vector.memset(row[:], 0.0)
+        def load_row(name, src, engine):
+            row = sb(name, UNITS, F32)
+            engine.memset(row[:], 0.0)
             nc.sync.dma_start(out=row[0:1, :], in_=src[0:1, :])
-        for t in range(2, PACK):
+            return row
+
+        wg_planes = plane_tiles("wg", "first")
+        load_plane(wg_planes, wg, 0)
+        for t in range(PACK):
+            nc.sync.dma_start(out=x_raw[:, t, :], in_=xT.rearrange("(p t) r -> p t r", t=PACK)[:, t, :])
+        tg_row = load_row("tg_row", tg, nc.vector)
+        tu_row = load_row("tu_row", tu, nc.gpsimd)
+        for t in range(1, PACK):
             load_plane(wg_planes, wg, t)
-        nc.sync.dma_start(out=x_raw[:], in_=xT.rearrange("(p t) r -> p t r", t=PACK))
-        wd_planes = load_planes("wd", wd, "second")
         nc.sync.dma_start(out=dy_raw[:], in_=dyT.rearrange("(p t) r -> p t r", t=PACK))
+        wd_planes = load_planes("wd", wd, "second")
 
         ident = sb("ident", P, F32)
         make_identity(nc, ident[:])
 
-        windows_1 = [sb("window_1_%d" % w, UNITS, F32) for w in range(2)]
-        for window in windows_1:
-            nc.vector.memset(window[:], 0.0)
+        def zeroed(name, engine, tag=None):
+            window = sb(name, UNITS, F32, tag)
+            engine.memset(window[:], 0.0)
+            return window
+
+        windows_1 = [zeroed("window_1_%d" % w, nc.vector) for w in range(2)]
+
+        def gather_scale(row, through, bank):
+            nc.vector.tensor_copy(through[:], row[:].indirect(offsets[:]))
+            for j in range(BLOCKS):
+                nc.tensor.transpose(bank[:, block(j)], through[:, block(j)], ident[:])
+            return bank[:, 0:512:P]
 
         staged = [sb("staged%d" % m, 512, F32) for m in range(BLOCKS)]
-        for n, row in enumerate((tg_row, tu_row)):
-            nc.vector.tensor_copy(staged[n][:], row[:].indirect(offsets[:]))
-            for j in range(BLOCKS):
-                nc.tensor.transpose(high[n][:, block(j)], staged[n][:, block(j)], ident[:])
+        wg_gathered = keep.tile([P, PACK, SLOTS], BF16, name="wg_gathered", align_bytes=64)
+        nc.vector.tensor_copy(wg_gathered[:, 0, :], wg_planes[0][:].indirect(offsets[:]))
+        tg_turned = gather_scale(tg_row, staged[0], high[0])
+        tu_turned = gather_scale(tu_row, staged[1], high[1])
         tg_col = sb("tg_col", BLOCKS, F32)
-        tg_neg_half = sb("tg_neg_half", BLOCKS, F32)
         tu_col = sb("tu_col", BLOCKS, F32)
         tg_tu = sb("tg_tu", BLOCKS, F32)
-        nc.scalar.copy(out=tg_col[:], in_=high[0][:, 0:512:P])
-        nc.scalar.mul(tg_neg_half[:], high[0][:, 0:512:P], -0.5)
-        nc.scalar.copy(out=tu_col[:], in_=high[1][:, 0:512:P])
-        nc.vector.tensor_tensor(tg_tu[:], tg_col[:], tu_col[:], ALU.mult)
+        tg_neg_half = sb("tg_neg_half", BLOCKS, F32)
+        nc.scalar.mul(tg_neg_half[:], tg_turned, -0.5)
+        nc.scalar.copy(out=tg_col[:], in_=tg_turned)
+        nc.scalar.copy(out=tu_col[:], in_=tu_turned)
         wt_us = sb("wt_us", BLOCKS, F32)
         wt_us_us = sb("wt_us_us", BLOCKS, F32)
-        nc.vector.tensor_tensor(wt_us[:], wt_col[:], us_col[:], ALU.mult)
-        nc.vector.tensor_tensor(wt_us_us[:], wt_us[:], us_col[:], ALU.mult)
-
-        windows_0 = [sb("window_0_0", UNITS, F32, "row0"), sb("window_0_1", UNITS, F32, "row1")]
-        for window in windows_0:
-            nc.gpsimd.memset(window[:], 0.0)
+        nc.gpsimd.tensor_tensor(wt_us[:], wt_col[:], us_col[:], ALU.mult)
+        nc.gpsimd.tensor_tensor(wt_us_us[:], wt_us[:], us_col[:], ALU.mult)
+        nc.gpsimd.tensor_tensor(tg_tu[:], tg_col[:], tu_col[:], ALU.mult)
+        windows_1.append(zeroed("window_1_2", nc.gpsimd, "tg_row"))
+        early_window_0 = zeroed("window_0_0", nc.gpsimd, "tu_row")
 
         def turn(src, bank, dst):
             words = src.bitcast(F32)
@@ -143,7 +155,7 @@ def tile_attend_gglu_w_kernel(tc, xT, wg, wu, dyT, wd, us, tg, tu, wt, offs, out
             return tile[:, 256 * j : 256 * (j + 1)]
 
         def gather(name, planes):
-            gathered = keep.tile([P, PACK, SLOTS], BF16, name=name)
+            gathered = keep.tile([P, PACK, SLOTS], BF16, name=name, align_bytes=64)
             for t in range(PACK):
                 nc.vector.tensor_copy(gathered[:, t, :], planes[t][:].indirect(offsets[:]))
             return gathered
@@ -154,15 +166,28 @@ def tile_attend_gglu_w_kernel(tc, xT, wg, wu, dyT, wd, us, tg, tu, wt, offs, out
                 for j in range(BLOCKS):
                     nc.tensor.transpose(dst_banks[j][:, block(m)], through[m][:, block(j)], ident[:])
 
-        wg_gathered = gather("wg_gathered", wg_planes)
-        wg_woven = sb("wg_woven", 2048, BF16)
-        weave(nc.scalar.copy, wg_woven[:], wg_gathered[:])
+        def weave_shared(dst, planes):
+            weave(nc.scalar.copy, dst[:, 0 : PACK * SCALAR_SLOTS], planes[:, :, 0:SCALAR_SLOTS])
+            weave(nc.vector.tensor_copy, dst[:, PACK * SCALAR_SLOTS :], planes[:, :, SCALAR_SLOTS:])
+
         x_woven = sb("x_woven", 2048, BF16)
-        weave(nc.vector.tensor_copy, x_woven[:], x_raw[:])
+        weave(nc.scalar.copy, x_woven[:], x_raw[:])
         x_d = mx_operand("x_d", E4M3)
         quantize(x_d, x_woven[:])
+        halves = [sb("half%d" % j, 1024, BF16) for j in range(BLOCKS)]
+        x_turned = sb("x_turned", 1024, F32)
+        for t in range(PACK):
+            nc.scalar.copy(out=halves[t][:, 0:512], in_=x_raw[:, t, :])
+            turn(halves[t][:, 0:512], low[t], turned(x_turned, t))
+
+        for t in range(1, PACK):
+            nc.vector.tensor_copy(wg_gathered[:, t, :], wg_planes[t][:].indirect(offsets[:]))
+        wg_woven = sb("wg_woven", 2048, BF16)
+        weave_shared(wg_woven, wg_gathered)
         wg_q = mx_operand("wg_q", E4M3)
         quantize(wg_q, wg_woven[:])
+        x_r = mx_operand("x_r", E4M3, "wg_woven")
+        quantize(x_r, x_turned[:].bitcast(BF16))
         wu_planes = load_planes("wu", wu, "first")
         for m in range(BLOCKS):
             product(low[m], x_d, m, wg_q)
@@ -171,41 +196,29 @@ def tile_attend_gglu_w_kernel(tc, xT, wg, wu, dyT, wd, us, tg, tu, wt, offs, out
         slope = [sb("slope%d" % j, 512, F32) for j in range(BLOCKS)]
         for j in range(BLOCKS):
             nc.scalar.activation(silu[j][:], high[j][:], ACT.Silu, scale=tg_col[:, j : j + 1])
-        for j in range(BLOCKS):
             nc.scalar.activation(slope[j][:], high[j][:], ACT.Tanh, scale=tg_neg_half[:, j : j + 1])
             nc.gpsimd.tensor_scalar(slope[j][:], slope[j][:], 0.5, 0.5, ALU.mult, ALU.add)
 
-        halves = [sb("half%d" % j, 512, BF16) for j in range(BLOCKS)]
-        x_turned = sb("x_turned", 1024, F32)
-        for t in range(PACK):
-            nc.scalar.copy(out=halves[t][:], in_=x_raw[:, t, :])
-            turn(halves[t][:], low[t], turned(x_turned, t))
-        x_r = mx_operand("x_r", E4M3)
-        quantize(x_r, x_turned[:].bitcast(BF16))
-
-        wd_gathered = gather("wd_gathered", wd_planes)
-        windows_0.append(sb("window_0_2", UNITS, F32, "second0"))
-        nc.gpsimd.memset(windows_0[2][:], 0.0)
-        wd_woven = sb("wd_woven", 2048, BF16)
-        weave(nc.scalar.copy, wd_woven[:, 0:1024], wd_gathered[:, :, 0:256])
-        weave(nc.vector.tensor_copy, wd_woven[:, 1024:2048], wd_gathered[:, :, 256:512])
-        wd_q = mx_operand("wd_q", E4M3)
-        quantize(wd_q, wd_woven[:])
         dy_woven = sb("dy_woven", 2048, BF16)
         dy_q = mx_operand("dy_q", E5M2)
         for m in range(BLOCKS):
-            copy = nc.scalar.copy if m == BLOCKS - 1 else nc.vector.tensor_copy
-            weave(copy, dy_woven[:, 512 * m : 512 * (m + 1)], dy_raw[:, :, block(m)])
+            weave(nc.scalar.copy, dy_woven[:, 512 * m : 512 * (m + 1)], dy_raw[:, :, block(m)])
+        quantize(dy_q, dy_woven[:])
+
+        wd_gathered = gather("wd_gathered", wd_planes)
+        wd_woven = sb("wd_woven", 2048, BF16)
+        weave_shared(wd_woven, wd_gathered)
+        wd_q = mx_operand("wd_q", E4M3)
+        quantize(wd_q, wd_woven[:])
         for m in range(BLOCKS):
-            quantize(dy_q, dy_woven[:, 512 * m : 512 * (m + 1)], block(m))
             product(low[m], dy_q, m, wd_q)
         scale_and_turn(low, wt_us, [s[:] for s in staged], high)
 
         du_turned = sb("du_turned", 1024, F32)
         du_q = mx_operand("du_q", E5M2)
         for j in range(BLOCKS):
-            nc.vector.scalar_tensor_tensor(halves[j][:], high[j][:], tu_col[:, j : j + 1], silu[j][:], ALU.mult, ALU.mult)
-            turn(halves[j][:], high[j], turned(du_turned, j))
+            nc.vector.scalar_tensor_tensor(halves[j][:, 0:512], high[j][:], tu_col[:, j : j + 1], silu[j][:], ALU.mult, ALU.mult)
+            turn(halves[j][:, 0:512], high[j], turned(du_turned, j))
         for j in range(BLOCKS):
             quantize(du_q, turned(du_turned, j).bitcast(BF16), block(j))
         for k in range(BLOCKS):
@@ -218,8 +231,6 @@ def tile_attend_gglu_w_kernel(tc, xT, wg, wu, dyT, wd, us, tg, tu, wt, offs, out
                 nc.tensor.transpose(low[j][:, block(m)], x_raw[:, m, block(j)], ident[:])
 
         wu_gathered = gather("wu_gathered", wu_planes)
-        wu_woven = sb("wu_woven", 2048, BF16)
-        weave(nc.scalar.copy, wu_woven[:], wu_gathered[:])
 
         for j in range(BLOCKS):
             nc.vector.scalar_tensor_tensor(slope[j][:], silu[j][:], -1.0, slope[j][:], ALU.add, ALU.mult)
@@ -234,21 +245,27 @@ def tile_attend_gglu_w_kernel(tc, xT, wg, wu, dyT, wd, us, tg, tu, wt, offs, out
         first_result = sb("first_result", 512, F32, "first3")
         put(high[0], first_result[:], windows_1[0], out_1, 0)
 
+        wu_woven = sb("wu_woven", 2048, BF16, "du_turned")
+        for j in range(BLOCKS):
+            weave(nc.scalar.copy, wu_woven[:, 512 * j : 512 * (j + 1)], wu_gathered[:, :, block(j)])
         wu_q = mx_operand("wu_q", E4M3)
         quantize(wu_q, wu_woven[:])
-        put(high[1], wu_woven[:, 0:1024].bitcast(F32), windows_1[1], out_1, 1)
+        second_result = sb("second_result", 512, F32, "wu_gathered")
+        put(high[1], second_result[:], windows_1[1], out_1, 1)
 
         for j in range(BLOCKS):
             product(low[j], wu_q, j, x_d)
         dg_turned = sb("dg_turned", 1024, F32)
         for j in range(BLOCKS):
-            nc.vector.scalar_tensor_tensor(halves[j][:], low[j][:], tg_tu[:, j : j + 1], slope[j][:], ALU.mult, ALU.mult)
-            turn(halves[j][:], low[j], turned(dg_turned, j))
-        put(high[2], slope[BLOCKS - 1][:], windows_1[0], out_1, 2)
+            nc.vector.scalar_tensor_tensor(halves[j][:, 0:512], low[j][:], tg_tu[:, j : j + 1], slope[j][:], ALU.mult, ALU.mult)
+        put(high[2], slope[2][:], windows_1[2], out_1, 2)
+        for j in range(BLOCKS):
+            turn(halves[j][:, 0:512], low[j], turned(dg_turned, j))
+        windows_0 = [early_window_0] + [zeroed("window_0_%d" % (j + 1), nc.gpsimd, "slope%d" % j) for j in range(2)]
 
         dg_q = mx_operand("dg_q", E5M2)
         quantize(dg_q, dg_turned[:].bitcast(BF16))
-        put(high[3], dg_turned[:, 0:512], windows_1[1], out_1, 3)
+        put(high[3], halves[3][:].bitcast(F32), windows_1[0], out_1, 3)
 
         for k in range(BLOCKS):
             product(low[k], x_r, k, dg_q)

@@ -66,11 +66,10 @@ def tile_attend_gglu_w_kernel(tc, xT, wg, wu, dyT, wd, us, tg, tu, wt, offs, out
         offsets = keep.tile([P, SLOTS // 16], U16, name="offsets")
         nc.sync.dma_start(offsets[:], offs)
 
-        us_col = sb("us_col", BLOCKS, F32)
-        wt_col = sb("wt_col", BLOCKS, F32)
-        with nc.allow_non_contiguous_dma(reason="one number a row, onto the partitions"):
-            nc.sync.dma_start(out=us_col[:], in_=us.rearrange("(m c) o -> c (m o)", c=P))
-            nc.sync.dma_start(out=wt_col[:], in_=wt.rearrange("(m c) o -> c (m o)", c=P))
+        row_factors = sb("row_factors", P, F32)
+        nc.gpsimd.memset(row_factors[:], 0.0)
+        nc.sync.dma_start(out=row_factors[0:BLOCKS, :], in_=us.rearrange("(m c) o -> m (c o)", c=P))
+        nc.sync.dma_start(out=row_factors[BLOCKS : 2 * BLOCKS, :], in_=wt.rearrange("(m c) o -> m (c o)", c=P))
         x_raw = keep.tile([P, PACK, R], F32, name="x_raw")
         dy_raw = keep.tile([P, PACK, R], F32, name="dy_raw")
 
@@ -97,13 +96,13 @@ def tile_attend_gglu_w_kernel(tc, xT, wg, wu, dyT, wd, us, tg, tu, wt, offs, out
 
         wg_planes = plane_tiles("wg", "first")
         load_plane(wg_planes, wg, 0)
-        for t in range(PACK):
-            nc.sync.dma_start(out=x_raw[:, t, :], in_=xT.rearrange("(p t) r -> p t r", t=PACK)[:, t, :])
+        for t in (0, 2):
+            nc.sync.dma_start(out=x_raw[:, t : t + 2, :], in_=xT.rearrange("(p t) r -> p t r", t=PACK)[:, t : t + 2, :])
         tg_row = load_row("tg_row", tg, nc.vector)
-        tu_row = load_row("tu_row", tu, nc.gpsimd)
         for t in range(1, PACK):
             load_plane(wg_planes, wg, t)
         nc.sync.dma_start(out=dy_raw[:], in_=dyT.rearrange("(p t) r -> p t r", t=PACK))
+        tu_row = load_row("tu_row", tu, nc.vector)
         wd_planes = load_planes("wd", wd, "second")
 
         ident = sb("ident", P, F32)
@@ -114,7 +113,9 @@ def tile_attend_gglu_w_kernel(tc, xT, wg, wu, dyT, wd, us, tg, tu, wt, offs, out
             engine.memset(window[:], 0.0)
             return window
 
+
         windows_1 = [zeroed("window_1_%d" % w, nc.vector) for w in range(2)]
+        windows_0 = [zeroed("window_0_%d" % w, nc.vector) for w in range(WINDOWS)]
 
         def gather_scale(row, through, bank):
             nc.vector.tensor_copy(through[:], row[:].indirect(offsets[:]))
@@ -124,23 +125,25 @@ def tile_attend_gglu_w_kernel(tc, xT, wg, wu, dyT, wd, us, tg, tu, wt, offs, out
 
         staged = [sb("staged%d" % m, 512, F32) for m in range(BLOCKS)]
         wg_gathered = keep.tile([P, PACK, SLOTS], BF16, name="wg_gathered", align_bytes=64)
-        nc.vector.tensor_copy(wg_gathered[:, 0, :], wg_planes[0][:].indirect(offsets[:]))
+        for t in range(2):
+            nc.vector.tensor_copy(wg_gathered[:, t, :], wg_planes[t][:].indirect(offsets[:]))
+        x_woven = sb("x_woven", 2048, BF16)
+        weave(nc.scalar.copy, x_woven[:], x_raw[:])
+        x_d = mx_operand("x_d", E4M3)
+        quantize(x_d, x_woven[:])
         tg_turned = gather_scale(tg_row, staged[0], high[0])
-        tu_turned = gather_scale(tu_row, staged[1], high[1])
         tg_col = sb("tg_col", BLOCKS, F32)
-        tu_col = sb("tu_col", BLOCKS, F32)
-        tg_tu = sb("tg_tu", BLOCKS, F32)
         tg_neg_half = sb("tg_neg_half", BLOCKS, F32)
         nc.scalar.mul(tg_neg_half[:], tg_turned, -0.5)
         nc.scalar.copy(out=tg_col[:], in_=tg_turned)
-        nc.scalar.copy(out=tu_col[:], in_=tu_turned)
+        nc.tensor.transpose(high[2][:, 0:P], row_factors[:], ident[:])
+        us_wt = sb("us_wt", 2 * BLOCKS, F32)
+        nc.scalar.copy(out=us_wt[:], in_=high[2][:, 0 : 2 * BLOCKS])
+        us_col, wt_col = us_wt[:, 0:BLOCKS], us_wt[:, BLOCKS:]
         wt_us = sb("wt_us", BLOCKS, F32)
         wt_us_us = sb("wt_us_us", BLOCKS, F32)
-        nc.gpsimd.tensor_tensor(wt_us[:], wt_col[:], us_col[:], ALU.mult)
-        nc.gpsimd.tensor_tensor(wt_us_us[:], wt_us[:], us_col[:], ALU.mult)
-        nc.gpsimd.tensor_tensor(tg_tu[:], tg_col[:], tu_col[:], ALU.mult)
-        windows_1.append(zeroed("window_1_2", nc.gpsimd, "tg_row"))
-        early_window_0 = zeroed("window_0_0", nc.gpsimd, "tu_row")
+        nc.gpsimd.tensor_tensor(wt_us[:], wt_col, us_col, ALU.mult)
+        nc.gpsimd.tensor_tensor(wt_us_us[:], wt_us[:], us_col, ALU.mult)
 
         def turn(src, bank, dst):
             words = src.bitcast(F32)
@@ -154,8 +157,8 @@ def tile_attend_gglu_w_kernel(tc, xT, wg, wu, dyT, wd, us, tg, tu, wt, offs, out
         def turned(tile, j):
             return tile[:, 256 * j : 256 * (j + 1)]
 
-        def gather(name, planes):
-            gathered = keep.tile([P, PACK, SLOTS], BF16, name=name, align_bytes=64)
+        def gather(name, planes, tag=None):
+            gathered = keep.tile([P, PACK, SLOTS], BF16, name=name, tag=tag or name, align_bytes=64)
             for t in range(PACK):
                 nc.vector.tensor_copy(gathered[:, t, :], planes[t][:].indirect(offsets[:]))
             return gathered
@@ -170,17 +173,13 @@ def tile_attend_gglu_w_kernel(tc, xT, wg, wu, dyT, wd, us, tg, tu, wt, offs, out
             weave(nc.scalar.copy, dst[:, 0 : PACK * SCALAR_SLOTS], planes[:, :, 0:SCALAR_SLOTS])
             weave(nc.vector.tensor_copy, dst[:, PACK * SCALAR_SLOTS :], planes[:, :, SCALAR_SLOTS:])
 
-        x_woven = sb("x_woven", 2048, BF16)
-        weave(nc.scalar.copy, x_woven[:], x_raw[:])
-        x_d = mx_operand("x_d", E4M3)
-        quantize(x_d, x_woven[:])
         halves = [sb("half%d" % j, 1024, BF16) for j in range(BLOCKS)]
         x_turned = sb("x_turned", 1024, F32)
         for t in range(PACK):
             nc.scalar.copy(out=halves[t][:, 0:512], in_=x_raw[:, t, :])
             turn(halves[t][:, 0:512], low[t], turned(x_turned, t))
 
-        for t in range(1, PACK):
+        for t in range(2, PACK):
             nc.vector.tensor_copy(wg_gathered[:, t, :], wg_planes[t][:].indirect(offsets[:]))
         wg_woven = sb("wg_woven", 2048, BF16)
         weave_shared(wg_woven, wg_gathered)
@@ -197,17 +196,25 @@ def tile_attend_gglu_w_kernel(tc, xT, wg, wu, dyT, wd, us, tg, tu, wt, offs, out
         for j in range(BLOCKS):
             nc.scalar.activation(silu[j][:], high[j][:], ACT.Silu, scale=tg_col[:, j : j + 1])
             nc.scalar.activation(slope[j][:], high[j][:], ACT.Tanh, scale=tg_neg_half[:, j : j + 1])
-            nc.gpsimd.tensor_scalar(slope[j][:], slope[j][:], 0.5, 0.5, ALU.mult, ALU.add)
 
-        dy_woven = sb("dy_woven", 2048, BF16)
+        dy_woven = sb("dy_woven", 2048, BF16, "wg_gathered")
         dy_q = mx_operand("dy_q", E5M2)
         for m in range(BLOCKS):
             weave(nc.scalar.copy, dy_woven[:, 512 * m : 512 * (m + 1)], dy_raw[:, :, block(m)])
         quantize(dy_q, dy_woven[:])
 
-        wd_gathered = gather("wd_gathered", wd_planes)
+        wd_gathered = gather("wd_gathered", wd_planes, "x_turned")
+        tu_gathered = sb("tu_gathered", 512, F32, "second0")
+        tu_turned = gather_scale(tu_row, tu_gathered, low[0])
+        tu_col = sb("tu_col", BLOCKS, F32)
+        tg_tu = sb("tg_tu", BLOCKS, F32)
+        nc.scalar.copy(out=tu_col[:], in_=tu_turned)
+        nc.gpsimd.tensor_tensor(tg_tu[:], tg_col[:], tu_col[:], ALU.mult)
+
         wd_woven = sb("wd_woven", 2048, BF16)
         weave_shared(wd_woven, wd_gathered)
+        for j in range(BLOCKS):
+            nc.scalar.activation(slope[j][:], slope[j][:], ACT.Identity, scale=0.5, bias=0.5)
         wd_q = mx_operand("wd_q", E4M3)
         quantize(wd_q, wd_woven[:])
         for m in range(BLOCKS):
@@ -230,7 +237,7 @@ def tile_attend_gglu_w_kernel(tc, xT, wg, wu, dyT, wd, us, tg, tu, wt, offs, out
             for j in range(BLOCKS):
                 nc.tensor.transpose(low[j][:, block(m)], x_raw[:, m, block(j)], ident[:])
 
-        wu_gathered = gather("wu_gathered", wu_planes)
+        wu_gathered = gather("wu_gathered", wu_planes, "wd_woven")
 
         for j in range(BLOCKS):
             nc.vector.scalar_tensor_tensor(slope[j][:], silu[j][:], -1.0, slope[j][:], ALU.add, ALU.mult)
@@ -250,7 +257,7 @@ def tile_attend_gglu_w_kernel(tc, xT, wg, wu, dyT, wd, us, tg, tu, wt, offs, out
             weave(nc.scalar.copy, wu_woven[:, 512 * j : 512 * (j + 1)], wu_gathered[:, :, block(j)])
         wu_q = mx_operand("wu_q", E4M3)
         quantize(wu_q, wu_woven[:])
-        second_result = sb("second_result", 512, F32, "wu_gathered")
+        second_result = sb("second_result", 512, F32, "wd_woven")
         put(high[1], second_result[:], windows_1[1], out_1, 1)
 
         for j in range(BLOCKS):
@@ -258,14 +265,13 @@ def tile_attend_gglu_w_kernel(tc, xT, wg, wu, dyT, wd, us, tg, tu, wt, offs, out
         dg_turned = sb("dg_turned", 1024, F32)
         for j in range(BLOCKS):
             nc.vector.scalar_tensor_tensor(halves[j][:, 0:512], low[j][:], tg_tu[:, j : j + 1], slope[j][:], ALU.mult, ALU.mult)
-        put(high[2], slope[2][:], windows_1[2], out_1, 2)
+        put(high[2], slope[2][:], windows_1[0], out_1, 2)
         for j in range(BLOCKS):
             turn(halves[j][:, 0:512], low[j], turned(dg_turned, j))
-        windows_0 = [early_window_0] + [zeroed("window_0_%d" % (j + 1), nc.gpsimd, "slope%d" % j) for j in range(2)]
 
-        dg_q = mx_operand("dg_q", E5M2)
+        dg_q = mx_operand("dg_q", E5M2, "slope2")
         quantize(dg_q, dg_turned[:].bitcast(BF16))
-        put(high[3], halves[3][:].bitcast(F32), windows_1[0], out_1, 3)
+        put(high[3], halves[3][:].bitcast(F32), windows_1[1], out_1, 3)
 
         for k in range(BLOCKS):
             product(low[k], x_r, k, dg_q)

@@ -3,8 +3,10 @@ from contextlib import ExitStack
 import concourse.mybir as mybir
 from concourse.masks import make_identity
 
-D, R, SLOTS, UNITS = 512, 512, 512, 2048
-FLOPS = 5 * 2 * 512 * 512 * 512
+K = 512
+UNITS = 2048
+FLOPS = 5 * 2 * K * K * K
+BYTES = 4 * (3 * K * UNITS + 2 * K * K + 2 * UNITS + 2 * K + 2 * K * UNITS) + 2 * 128 * (K // 16)
 
 F32 = mybir.dt.float32
 BF16 = mybir.dt.bfloat16
@@ -18,13 +20,18 @@ ACT = mybir.ActivationFunctionType
 
 P = 128
 PACK = 4
-BLOCKS = 4
-WINDOWS = 3
+BLOCKS = K // P
+PAIRS = K // 2
+WINDOWS_1, WINDOWS_0 = 2, 3
 SCALAR_SLOTS = 192
 
 
 def block(b):
     return slice(b * P, (b + 1) * P)
+
+
+def by_plane(matrix):
+    return matrix.rearrange("(p t) c -> p t c", t=PACK)
 
 
 def tile_attend_gglu_w_kernel(tc, xT, wg, wu, dyT, wd, us, tg, tu, wt, offs, out_0, out_1):
@@ -36,12 +43,21 @@ def tile_attend_gglu_w_kernel(tc, xT, wg, wu, dyT, wd, us, tg, tu, wt, offs, out
         def sb(name, cols, dtype, tag=None):
             return keep.tile([P, cols], dtype, name=name, tag=tag or name, align_bytes=64)
 
-        def mx_operand(name, fmt, tag=None):
-            return sb(name + "_codes", 512, U32, tag), sb(name + "_scales", 512, U8), fmt
+        def sb_planes(name, dtype, tag=None):
+            return keep.tile([P, PACK, K], dtype, name=name, tag=tag or name, align_bytes=64)
 
-        def quantize(operand, src, cols=slice(0, 512)):
+        banks = [psum.tile([P, K], F32, name="bank%d" % b) for b in range(2 * BLOCKS)]
+        low, high = banks[:BLOCKS], banks[BLOCKS:]
+
+        offsets = keep.tile([P, K // 16], U16, name="offsets")
+        nc.sync.dma_start(offsets[:], offs)
+
+        def mx_operand(name, fmt, tag=None):
+            return sb(name + "_codes", K, U32, tag), sb(name + "_scales", K, U8), fmt
+
+        def quantize(operand, woven, cols=slice(0, K)):
             codes, scales, fmt = operand
-            nc.vector.quantize_mx(out=codes[:, cols].bitcast(fmt), scales=scales[:, cols], in_=src)
+            nc.vector.quantize_mx(out=codes[:, cols].bitcast(fmt), scales=scales[:, cols], in_=woven)
 
         def product(bank, stationary, b, moving):
             nc.tensor.matmul_mx(
@@ -54,83 +70,93 @@ def tile_attend_gglu_w_kernel(tc, xT, wg, wu, dyT, wd, us, tg, tu, wt, offs, out
                 stop=True,
             )
 
-        def weave(engine_copy, dst, planes):
-            engine_copy(
-                out=dst.rearrange("p (c i t) -> p c t i", i=4, t=PACK),
+        def weave(copy, woven, planes):
+            copy(
+                out=woven.rearrange("p (c i t) -> p c t i", i=4, t=PACK),
                 in_=planes.rearrange("p t (c i) -> p c t i", i=4),
             )
 
-        banks = [psum.tile([P, 512], F32, name="bank%d" % b) for b in range(8)]
-        low, high = banks[:4], banks[4:]
+        def woven_block(woven, b):
+            return woven[:, PACK * P * b : PACK * P * (b + 1)]
 
-        offsets = keep.tile([P, SLOTS // 16], U16, name="offsets")
-        nc.sync.dma_start(offsets[:], offs)
-
-        row_factors = sb("row_factors", P, F32)
-        nc.gpsimd.memset(row_factors[:], 0.0)
-        nc.sync.dma_start(out=row_factors[0:BLOCKS, :], in_=us.rearrange("(m c) o -> m (c o)", c=P))
-        nc.sync.dma_start(out=row_factors[BLOCKS : 2 * BLOCKS, :], in_=wt.rearrange("(m c) o -> m (c o)", c=P))
-        x_raw = keep.tile([P, PACK, R], F32, name="x_raw")
-        dy_raw = keep.tile([P, PACK, R], F32, name="dy_raw")
-
-        def plane_tiles(name, tag):
-            return [sb("%s%d" % (name, t), UNITS, F32, "%s%d" % (tag, t)) for t in range(PACK)]
-
-        def load_plane(planes, matrix, t, pieces=1):
-            width = UNITS // pieces
-            for q in range(pieces):
-                cols = slice(width * q, width * (q + 1))
-                nc.sync.dma_start(out=planes[t][:, cols], in_=matrix.rearrange("(p t) c -> p t c", t=PACK)[:, t, cols])
-
-        def load_planes(name, matrix, tag):
-            planes = plane_tiles(name, tag)
-            for t in range(PACK):
-                load_plane(planes, matrix, t)
-            return planes
-
-        def load_row(name, src, engine):
-            row = sb(name, UNITS, F32)
-            engine.memset(row[:], 0.0)
-            nc.sync.dma_start(out=row[0:1, :], in_=src[0:1, :])
-            return row
-
-        wg_planes = plane_tiles("wg", "first")
-        load_plane(wg_planes, wg, 0)
-        for t in (0, 2):
-            nc.sync.dma_start(out=x_raw[:, t : t + 2, :], in_=xT.rearrange("(p t) r -> p t r", t=PACK)[:, t : t + 2, :])
-        tg_row = load_row("tg_row", tg, nc.vector)
-        for t in range(1, PACK):
-            load_plane(wg_planes, wg, t)
-        nc.sync.dma_start(out=dy_raw[:], in_=dyT.rearrange("(p t) r -> p t r", t=PACK))
-        tu_row = load_row("tu_row", tu, nc.vector)
-        wd_planes = load_planes("wd", wd, "second")
-
-        ident = sb("ident", P, F32)
-        make_identity(nc, ident[:])
-
-        def zeroed(name, engine, tag=None):
-            window = sb(name, UNITS, F32, tag)
-            engine.memset(window[:], 0.0)
-            return window
-
-
-        windows_1 = [zeroed("window_1_%d" % w, nc.vector) for w in range(2)]
-        windows_0 = [zeroed("window_0_%d" % w, nc.vector) for w in range(WINDOWS)]
+        def gather_planes(gathered, windows, planes):
+            for t in planes:
+                nc.vector.tensor_copy(gathered[:, t, :], windows[t][:].indirect(offsets[:]))
 
         def gather_scale(row, through, bank):
             nc.vector.tensor_copy(through[:], row[:].indirect(offsets[:]))
             for j in range(BLOCKS):
                 nc.tensor.transpose(bank[:, block(j)], through[:, block(j)], ident[:])
-            return bank[:, 0:512:P]
+            return bank[:, 0:K:P]
 
-        staged = [sb("staged%d" % m, 512, F32) for m in range(BLOCKS)]
-        wg_gathered = keep.tile([P, PACK, SLOTS], BF16, name="wg_gathered", align_bytes=64)
-        for t in range(2):
-            nc.vector.tensor_copy(wg_gathered[:, t, :], wg_planes[t][:].indirect(offsets[:]))
-        x_woven = sb("x_woven", 2048, BF16)
+        def scale_and_turn(src_banks, row_factor):
+            for m in range(BLOCKS):
+                nc.scalar.activation(staged[m][:], src_banks[m][:], ACT.Copy, scale=row_factor[:, m : m + 1])
+                for j in range(BLOCKS):
+                    nc.tensor.transpose(high[j][:, block(m)], staged[m][:, block(j)], ident[:])
+
+        def rows_to_partitions(j, bank, turned):
+            words = rounded[j][:, 0:K].bitcast(F32)
+            for u in range(2):
+                nc.tensor.transpose(bank[:, block(u)], words[:, u:PAIRS:2], ident[:])
+            nc.scalar.copy(
+                out=turned[:, PAIRS * j : PAIRS * (j + 1)].rearrange("p (c u) -> p c u", u=2),
+                in_=bank[:, 0:PAIRS].rearrange("p (u c) -> p c u", u=2),
+            )
+
+        def put(bank, through, window, out, k):
+            nc.scalar.copy(out=through, in_=bank[:])
+            nc.vector.tensor_copy(window[:].indirect(offsets[:]), through)
+            nc.sync.dma_start(out=by_plane(out)[:, k, :], in_=window[:])
+
+        row_factors = sb("row_factors", P, F32)
+        nc.gpsimd.memset(row_factors[:], 0.0)
+        nc.sync.dma_start(out=row_factors[0:BLOCKS, :], in_=us.rearrange("(m c) o -> m (c o)", c=P))
+        nc.sync.dma_start(out=row_factors[BLOCKS : 2 * BLOCKS, :], in_=wt.rearrange("(m c) o -> m (c o)", c=P))
+        ident = sb("ident", P, F32)
+        make_identity(nc, ident[:])
+
+        def plane_windows(name, tag):
+            return [sb("%s%d" % (name, t), UNITS, F32, "%s%d" % (tag, t)) for t in range(PACK)]
+
+        def load_planes(windows, matrix, planes):
+            for t in planes:
+                nc.sync.dma_start(out=windows[t][:], in_=by_plane(matrix)[:, t, :])
+
+        def zeroed(name):
+            window = sb(name, UNITS, F32)
+            nc.vector.memset(window[:], 0.0)
+            return window
+
+        def load_row(name, scale):
+            row = zeroed(name)
+            nc.sync.dma_start(out=row[0:1, :], in_=scale[0:1, :])
+            return row
+
+        x_raw = sb_planes("x_raw", F32)
+        dy_raw = sb_planes("dy_raw", F32)
+        wg_windows = plane_windows("wg", "wg_then_wu")
+        wd_windows = plane_windows("wd", "wd")
+        load_planes(wg_windows, wg, range(1))
+        for t in range(0, PACK, 2):
+            nc.sync.dma_start(out=x_raw[:, t : t + 2, :], in_=by_plane(xT)[:, t : t + 2, :])
+        tg_row = load_row("tg_row", tg)
+        load_planes(wg_windows, wg, range(1, PACK))
+        nc.sync.dma_start(out=dy_raw[:], in_=by_plane(dyT))
+        tu_row = load_row("tu_row", tu)
+        load_planes(wd_windows, wd, range(PACK))
+
+        windows_1 = [zeroed("window_1_%d" % w) for w in range(WINDOWS_1)]
+        windows_0 = [zeroed("window_0_%d" % w) for w in range(WINDOWS_0)]
+
+        staged = [sb("staged%d" % m, K, F32) for m in range(BLOCKS)]
+        wg_gathered = sb_planes("wg_gathered", BF16)
+        gather_planes(wg_gathered, wg_windows, range(2))
+        x_woven = sb("x_woven", PACK * K, BF16)
         weave(nc.scalar.copy, x_woven[:], x_raw[:])
-        x_d = mx_operand("x_d", E4M3)
-        quantize(x_d, x_woven[:])
+        x_along_d = mx_operand("x_along_d", E4M3)
+        quantize(x_along_d, x_woven[:])
+
         tg_turned = gather_scale(tg_row, staged[0], high[0])
         tg_col = sb("tg_col", BLOCKS, F32)
         tg_neg_half = sb("tg_neg_half", BLOCKS, F32)
@@ -141,138 +167,105 @@ def tile_attend_gglu_w_kernel(tc, xT, wg, wu, dyT, wd, us, tg, tu, wt, offs, out
         nc.scalar.copy(out=us_wt[:], in_=high[2][:, 0 : 2 * BLOCKS])
         us_col, wt_col = us_wt[:, 0:BLOCKS], us_wt[:, BLOCKS:]
         wt_us = sb("wt_us", BLOCKS, F32)
-        wt_us_us = sb("wt_us_us", BLOCKS, F32)
         nc.gpsimd.tensor_tensor(wt_us[:], wt_col, us_col, ALU.mult)
-        nc.gpsimd.tensor_tensor(wt_us_us[:], wt_us[:], us_col, ALU.mult)
 
-        def turn(src, bank, dst):
-            words = src.bitcast(F32)
-            for u in range(2):
-                nc.tensor.transpose(bank[:, block(u)], words[:, u:256:2], ident[:])
-            nc.scalar.copy(
-                out=dst.rearrange("p (c u) -> p c u", u=2),
-                in_=bank[:, 0:256].rearrange("p (u c) -> p c u", u=2),
-            )
-
-        def turned(tile, j):
-            return tile[:, 256 * j : 256 * (j + 1)]
-
-        def gather(name, planes, tag=None):
-            gathered = keep.tile([P, PACK, SLOTS], BF16, name=name, tag=tag or name, align_bytes=64)
-            for t in range(PACK):
-                nc.vector.tensor_copy(gathered[:, t, :], planes[t][:].indirect(offsets[:]))
-            return gathered
-
-        def scale_and_turn(src_banks, scale, through, dst_banks):
-            for m in range(BLOCKS):
-                nc.scalar.activation(through[m], src_banks[m][:], ACT.Copy, scale=scale[:, m : m + 1])
-                for j in range(BLOCKS):
-                    nc.tensor.transpose(dst_banks[j][:, block(m)], through[m][:, block(j)], ident[:])
-
-        def weave_shared(dst, planes):
-            weave(nc.scalar.copy, dst[:, 0 : PACK * SCALAR_SLOTS], planes[:, :, 0:SCALAR_SLOTS])
-            weave(nc.vector.tensor_copy, dst[:, PACK * SCALAR_SLOTS :], planes[:, :, SCALAR_SLOTS:])
-
-        halves = [sb("half%d" % j, 1024, BF16) for j in range(BLOCKS)]
-        x_turned = sb("x_turned", 1024, F32)
+        rounded = [sb("rounded%d" % j, 2 * K, BF16) for j in range(BLOCKS)]
+        x_turned = sb("x_turned", 2 * K, F32)
         for t in range(PACK):
-            nc.scalar.copy(out=halves[t][:, 0:512], in_=x_raw[:, t, :])
-            turn(halves[t][:, 0:512], low[t], turned(x_turned, t))
+            nc.scalar.copy(out=rounded[t][:, 0:K], in_=x_raw[:, t, :])
+            rows_to_partitions(t, low[t], x_turned)
 
-        for t in range(2, PACK):
-            nc.vector.tensor_copy(wg_gathered[:, t, :], wg_planes[t][:].indirect(offsets[:]))
-        wg_woven = sb("wg_woven", 2048, BF16)
-        weave_shared(wg_woven, wg_gathered)
+        gather_planes(wg_gathered, wg_windows, range(2, PACK))
+        wg_woven = sb("wg_woven", PACK * K, BF16)
+        weave(nc.scalar.copy, wg_woven[:, 0 : PACK * SCALAR_SLOTS], wg_gathered[:, :, 0:SCALAR_SLOTS])
+        weave(nc.vector.tensor_copy, wg_woven[:, PACK * SCALAR_SLOTS :], wg_gathered[:, :, SCALAR_SLOTS:])
         wg_q = mx_operand("wg_q", E4M3)
         quantize(wg_q, wg_woven[:])
-        x_r = mx_operand("x_r", E4M3, "wg_woven")
-        quantize(x_r, x_turned[:].bitcast(BF16))
-        wu_planes = load_planes("wu", wu, "first")
+        x_along_r = mx_operand("x_along_r", E4M3, tag="wg_woven")
+        quantize(x_along_r, x_turned[:].bitcast(BF16))
+
+        dy_woven = sb("dy_woven", PACK * K, BF16, tag="wg_gathered")
+        dy_q = mx_operand("dy_q", E5M2)
         for m in range(BLOCKS):
-            product(low[m], x_d, m, wg_q)
-        scale_and_turn(low, us_col, [s[:] for s in staged], high)
-        silu = [sb("silu%d" % j, 512, F32) for j in range(BLOCKS)]
-        slope = [sb("slope%d" % j, 512, F32) for j in range(BLOCKS)]
+            weave(nc.scalar.copy, woven_block(dy_woven, m), dy_raw[:, :, block(m)])
+        quantize(dy_q, dy_woven[:])
+
+        wu_windows = plane_windows("wu", "wg_then_wu")
+        load_planes(wu_windows, wu, range(PACK))
+        for m in range(BLOCKS):
+            product(low[m], x_along_d, m, wg_q)
+        scale_and_turn(low, us_col)
+        silu = [sb("silu%d" % j, K, F32) for j in range(BLOCKS)]
+        slope = [sb("slope%d" % j, K, F32) for j in range(BLOCKS)]
         for j in range(BLOCKS):
             nc.scalar.activation(silu[j][:], high[j][:], ACT.Silu, scale=tg_col[:, j : j + 1])
             nc.scalar.activation(slope[j][:], high[j][:], ACT.Tanh, scale=tg_neg_half[:, j : j + 1])
 
-        dy_woven = sb("dy_woven", 2048, BF16, "wg_gathered")
-        dy_q = mx_operand("dy_q", E5M2)
-        for m in range(BLOCKS):
-            weave(nc.scalar.copy, dy_woven[:, 512 * m : 512 * (m + 1)], dy_raw[:, :, block(m)])
-        quantize(dy_q, dy_woven[:])
-
-        wd_gathered = gather("wd_gathered", wd_planes, "x_turned")
-        tu_gathered = sb("tu_gathered", 512, F32, "second0")
+        wd_gathered = sb_planes("wd_gathered", BF16, tag="x_turned")
+        gather_planes(wd_gathered, wd_windows, range(PACK))
+        tu_gathered = sb("tu_gathered", K, F32, tag="wd0")
         tu_turned = gather_scale(tu_row, tu_gathered, low[0])
         tu_col = sb("tu_col", BLOCKS, F32)
         tg_tu = sb("tg_tu", BLOCKS, F32)
         nc.scalar.copy(out=tu_col[:], in_=tu_turned)
         nc.gpsimd.tensor_tensor(tg_tu[:], tg_col[:], tu_col[:], ALU.mult)
 
-        wd_woven = sb("wd_woven", 2048, BF16)
-        weave_shared(wd_woven, wd_gathered)
-        for j in range(BLOCKS):
-            nc.scalar.activation(slope[j][:], slope[j][:], ACT.Identity, scale=0.5, bias=0.5)
+        wd_woven = sb("wd_woven", PACK * K, BF16)
+        weave(nc.vector.tensor_copy, wd_woven[:], wd_gathered[:])
         wd_q = mx_operand("wd_q", E4M3)
         quantize(wd_q, wd_woven[:])
         for m in range(BLOCKS):
             product(low[m], dy_q, m, wd_q)
-        scale_and_turn(low, wt_us, [s[:] for s in staged], high)
+        scale_and_turn(low, wt_us)
 
-        du_turned = sb("du_turned", 1024, F32)
+        one_less_s = sb_planes("one_less_s", F32, tag="x_turned")
+        for j in range(BLOCKS):
+            nc.scalar.activation(one_less_s[:, j, :], slope[j][:], ACT.Identity, scale=0.5, bias=0.5)
+            nc.vector.scalar_tensor_tensor(slope[j][:], silu[j][:], -1.0, one_less_s[:, j, :], ALU.add, ALU.mult)
+
+        du_turned = sb("du_turned", 2 * K, F32)
         du_q = mx_operand("du_q", E5M2)
         for j in range(BLOCKS):
-            nc.vector.scalar_tensor_tensor(halves[j][:, 0:512], high[j][:], tu_col[:, j : j + 1], silu[j][:], ALU.mult, ALU.mult)
-            turn(halves[j][:, 0:512], high[j], turned(du_turned, j))
+            nc.vector.scalar_tensor_tensor(
+                rounded[j][:, 0:K], high[j][:], tu_col[:, j : j + 1], silu[j][:], ALU.mult, ALU.mult
+            )
+            rows_to_partitions(j, low[j], du_turned)
         for j in range(BLOCKS):
-            quantize(du_q, turned(du_turned, j).bitcast(BF16), block(j))
-        for k in range(BLOCKS):
-            product(high[k], x_r, k, du_q)
+            quantize(du_q, du_turned[:, PAIRS * j : PAIRS * (j + 1)].bitcast(BF16), block(j))
+        for k in range(WINDOWS_1):
+            product(low[k], x_along_r, k, du_q)
 
-        for m in range(BLOCKS):
-            nc.scalar.activation(x_raw[:, m, :], low[m][:], ACT.Copy, scale=wt_us_us[:, m : m + 1])
-        for m in range(BLOCKS):
-            for j in range(BLOCKS):
-                nc.tensor.transpose(low[j][:, block(m)], x_raw[:, m, block(j)], ident[:])
-
-        wu_gathered = gather("wu_gathered", wu_planes, "wd_woven")
-
+        wu_gathered = sb_planes("wu_gathered", BF16, tag="wd_woven")
+        gather_planes(wu_gathered, wu_windows, range(PACK))
+        wu_woven = sb("wu_woven", PACK * K, BF16)
         for j in range(BLOCKS):
-            nc.vector.scalar_tensor_tensor(slope[j][:], silu[j][:], -1.0, slope[j][:], ALU.add, ALU.mult)
-        for j in range(BLOCKS):
-            nc.vector.scalar_tensor_tensor(slope[j][:], slope[j][:], 1.0, low[j][:], ALU.add, ALU.mult)
-
-        def put(bank, through, window, out, k):
-            nc.scalar.copy(out=through, in_=bank[:])
-            nc.vector.tensor_copy(window[:].indirect(offsets[:]), through)
-            nc.sync.dma_start(out=out.rearrange("(p t) c -> p t c", t=PACK)[:, k, :], in_=window[:])
-
-        first_result = sb("first_result", 512, F32, "first3")
-        put(high[0], first_result[:], windows_1[0], out_1, 0)
-
-        wu_woven = sb("wu_woven", 2048, BF16, "du_turned")
-        for j in range(BLOCKS):
-            weave(nc.scalar.copy, wu_woven[:, 512 * j : 512 * (j + 1)], wu_gathered[:, :, block(j)])
+            weave(nc.scalar.copy, woven_block(wu_woven, j), wu_gathered[:, :, block(j)])
         wu_q = mx_operand("wu_q", E4M3)
         quantize(wu_q, wu_woven[:])
-        second_result = sb("second_result", 512, F32, "wd_woven")
-        put(high[1], second_result[:], windows_1[1], out_1, 1)
+        for j in range(BLOCKS):
+            nc.vector.scalar_tensor_tensor(slope[j][:], slope[j][:], 1.0, high[j][:], ALU.add, ALU.mult)
 
-        for j in range(BLOCKS):
-            product(low[j], wu_q, j, x_d)
-        dg_turned = sb("dg_turned", 1024, F32)
-        for j in range(BLOCKS):
-            nc.vector.scalar_tensor_tensor(halves[j][:, 0:512], low[j][:], tg_tu[:, j : j + 1], slope[j][:], ALU.mult, ALU.mult)
-        put(high[2], slope[2][:], windows_1[0], out_1, 2)
-        for j in range(BLOCKS):
-            turn(halves[j][:, 0:512], low[j], turned(dg_turned, j))
+        for k in range(WINDOWS_1):
+            put(low[k], silu[k][:], windows_1[k], out_1, k)
 
-        dg_q = mx_operand("dg_q", E5M2, "slope2")
+        free_first = low[WINDOWS_1:] + low[:WINDOWS_1]
+        for m in range(BLOCKS):
+            product(free_first[m], x_along_d, m, wu_q)
+        scale_and_turn(free_first, us_col)
+        for k in range(WINDOWS_1, BLOCKS):
+            product(low[k], x_along_r, k, du_q)
+        for j in range(BLOCKS):
+            nc.vector.scalar_tensor_tensor(
+                rounded[j][:, 0:K], high[j][:], tg_tu[:, j : j + 1], slope[j][:], ALU.mult, ALU.mult
+            )
+        put(low[2], slope[2][:], windows_1[0], out_1, 2)
+        dg_turned = sb("dg_turned", 2 * K, F32)
+        for j in range(BLOCKS):
+            rows_to_partitions(j, high[j], dg_turned)
+        dg_q = mx_operand("dg_q", E5M2, tag="slope2")
         quantize(dg_q, dg_turned[:].bitcast(BF16))
-        put(high[3], halves[3][:].bitcast(F32), windows_1[1], out_1, 3)
+        put(low[3], rounded[3][:].bitcast(F32), windows_1[1], out_1, 3)
 
         for k in range(BLOCKS):
-            product(low[k], x_r, k, dg_q)
-            put(low[k], staged[k][:], windows_0[k % WINDOWS], out_0, k)
+            product(high[k], x_along_r, k, dg_q)
+            put(high[k], staged[k][:], windows_0[k % WINDOWS_0], out_0, k)

from contextlib import ExitStack

import concourse.mybir as mybir
from concourse.masks import make_identity

K = 512
UNITS = 2048
FLOPS = 5 * 2 * K * K * K
BYTES = 4 * (3 * K * UNITS + 2 * K * K + 2 * UNITS + 2 * K + 2 * K * UNITS) + 2 * 128 * (K // 16)

F32 = mybir.dt.float32
BF16 = mybir.dt.bfloat16
U32 = mybir.dt.uint32
U16 = mybir.dt.uint16
U8 = mybir.dt.uint8
E4M3 = mybir.dt.float8_e4m3fn_x4
E5M2 = mybir.dt.float8_e5m2_x4
ALU = mybir.AluOpType
ACT = mybir.ActivationFunctionType

P = 128
PACK = 4
BLOCKS = K // P
PAIRS = K // 2
WINDOWS_1, WINDOWS_0 = 2, 3
SCALAR_SLOTS = 192


def block(b):
    return slice(b * P, (b + 1) * P)


def by_plane(matrix):
    return matrix.rearrange("(p t) c -> p t c", t=PACK)


def tile_attend_gglu_w_kernel(tc, xT, wg, wu, dyT, wd, us, tg, tu, wt, offs, out_0, out_1):
    nc = tc.nc
    with ExitStack() as ctx:
        keep = ctx.enter_context(tc.tile_pool(name="keep", bufs=1))
        psum = ctx.enter_context(tc.psum_pool(name="psum", bufs=1))

        def sb(name, cols, dtype, tag=None):
            return keep.tile([P, cols], dtype, name=name, tag=tag or name, align_bytes=64)

        def sb_planes(name, dtype, tag=None):
            return keep.tile([P, PACK, K], dtype, name=name, tag=tag or name, align_bytes=64)

        banks = [psum.tile([P, K], F32, name="bank%d" % b) for b in range(2 * BLOCKS)]
        low, high = banks[:BLOCKS], banks[BLOCKS:]

        offsets = keep.tile([P, K // 16], U16, name="offsets")
        nc.sync.dma_start(offsets[:], offs)

        def mx_operand(name, fmt, tag=None):
            return sb(name + "_codes", K, U32, tag), sb(name + "_scales", K, U8), fmt

        def quantize(operand, woven, cols=slice(0, K)):
            codes, scales, fmt = operand
            nc.vector.quantize_mx(out=codes[:, cols].bitcast(fmt), scales=scales[:, cols], in_=woven)

        def product(bank, stationary, b, moving):
            nc.tensor.matmul_mx(
                out=bank[:],
                lhsT=stationary[0][:, block(b)].bitcast(stationary[2]),
                lhsT_scale=stationary[1][:, block(b)],
                rhs=moving[0][:].bitcast(moving[2]),
                rhs_scale=moving[1][:],
                start=True,
                stop=True,
            )

        def weave(copy, woven, planes):
            copy(
                out=woven.rearrange("p (c i t) -> p c t i", i=4, t=PACK),
                in_=planes.rearrange("p t (c i) -> p c t i", i=4),
            )

        def woven_block(woven, b):
            return woven[:, PACK * P * b : PACK * P * (b + 1)]

        def gather_planes(gathered, windows, planes):
            for t in planes:
                nc.vector.tensor_copy(gathered[:, t, :], windows[t][:].indirect(offsets[:]))

        def gather_scale(row, through, bank):
            nc.vector.tensor_copy(through[:], row[:].indirect(offsets[:]))
            for j in range(BLOCKS):
                nc.tensor.transpose(bank[:, block(j)], through[:, block(j)], ident[:])
            return bank[:, 0:K:P]

        def scale_and_turn(src_banks, row_factor):
            for m in range(BLOCKS):
                nc.scalar.activation(staged[m][:], src_banks[m][:], ACT.Copy, scale=row_factor[:, m : m + 1])
                for j in range(BLOCKS):
                    nc.tensor.transpose(high[j][:, block(m)], staged[m][:, block(j)], ident[:])

        def rows_to_partitions(j, bank, turned):
            words = rounded[j][:, 0:K].bitcast(F32)
            for u in range(2):
                nc.tensor.transpose(bank[:, block(u)], words[:, u:PAIRS:2], ident[:])
            nc.scalar.copy(
                out=turned[:, PAIRS * j : PAIRS * (j + 1)].rearrange("p (c u) -> p c u", u=2),
                in_=bank[:, 0:PAIRS].rearrange("p (u c) -> p c u", u=2),
            )

        def put(bank, through, window, out, k):
            nc.scalar.copy(out=through, in_=bank[:])
            nc.vector.tensor_copy(window[:].indirect(offsets[:]), through)
            nc.sync.dma_start(out=by_plane(out)[:, k, :], in_=window[:])

        row_factors = sb("row_factors", P, F32)
        nc.gpsimd.memset(row_factors[:], 0.0)
        nc.sync.dma_start(out=row_factors[0:BLOCKS, :], in_=us.rearrange("(m c) o -> m (c o)", c=P))
        nc.sync.dma_start(out=row_factors[BLOCKS : 2 * BLOCKS, :], in_=wt.rearrange("(m c) o -> m (c o)", c=P))
        ident = sb("ident", P, F32)
        make_identity(nc, ident[:])

        def plane_windows(name, tag):
            return [sb("%s%d" % (name, t), UNITS, F32, "%s%d" % (tag, t)) for t in range(PACK)]

        def load_planes(windows, matrix, planes):
            for t in planes:
                nc.sync.dma_start(out=windows[t][:], in_=by_plane(matrix)[:, t, :])

        def zeroed(name):
            window = sb(name, UNITS, F32)
            nc.vector.memset(window[:], 0.0)
            return window

        def load_row(name, scale):
            row = zeroed(name)
            nc.sync.dma_start(out=row[0:1, :], in_=scale[0:1, :])
            return row

        x_raw = sb_planes("x_raw", F32)
        dy_raw = sb_planes("dy_raw", F32)
        wg_windows = plane_windows("wg", "wg_then_wu")
        wd_windows = plane_windows("wd", "wd")
        load_planes(wg_windows, wg, range(1))
        for t in range(0, PACK, 2):
            nc.sync.dma_start(out=x_raw[:, t : t + 2, :], in_=by_plane(xT)[:, t : t + 2, :])
        tg_row = load_row("tg_row", tg)
        load_planes(wg_windows, wg, range(1, PACK))
        nc.sync.dma_start(out=dy_raw[:], in_=by_plane(dyT))
        tu_row = load_row("tu_row", tu)
        load_planes(wd_windows, wd, range(PACK))

        windows_1 = [zeroed("window_1_%d" % w) for w in range(WINDOWS_1)]
        windows_0 = [zeroed("window_0_%d" % w) for w in range(WINDOWS_0)]

        staged = [sb("staged%d" % m, K, F32) for m in range(BLOCKS)]
        wg_gathered = sb_planes("wg_gathered", BF16)
        gather_planes(wg_gathered, wg_windows, range(2))
        x_woven = sb("x_woven", PACK * K, BF16)
        weave(nc.scalar.copy, x_woven[:], x_raw[:])
        x_along_d = mx_operand("x_along_d", E4M3)
        quantize(x_along_d, x_woven[:])

        tg_turned = gather_scale(tg_row, staged[0], high[0])
        tg_col = sb("tg_col", BLOCKS, F32)
        tg_neg_half = sb("tg_neg_half", BLOCKS, F32)
        nc.scalar.mul(tg_neg_half[:], tg_turned, -0.5)
        nc.scalar.copy(out=tg_col[:], in_=tg_turned)
        nc.tensor.transpose(high[2][:, 0:P], row_factors[:], ident[:])
        us_wt = sb("us_wt", 2 * BLOCKS, F32)
        nc.scalar.copy(out=us_wt[:], in_=high[2][:, 0 : 2 * BLOCKS])
        us_col, wt_col = us_wt[:, 0:BLOCKS], us_wt[:, BLOCKS:]
        wt_us = sb("wt_us", BLOCKS, F32)
        nc.gpsimd.tensor_tensor(wt_us[:], wt_col, us_col, ALU.mult)

        rounded = [sb("rounded%d" % j, 2 * K, BF16) for j in range(BLOCKS)]
        x_turned = sb("x_turned", 2 * K, F32)
        for t in range(PACK):
            nc.scalar.copy(out=rounded[t][:, 0:K], in_=x_raw[:, t, :])
            rows_to_partitions(t, low[t], x_turned)

        gather_planes(wg_gathered, wg_windows, range(2, PACK))
        wg_woven = sb("wg_woven", PACK * K, BF16)
        weave(nc.scalar.copy, wg_woven[:, 0 : PACK * SCALAR_SLOTS], wg_gathered[:, :, 0:SCALAR_SLOTS])
        weave(nc.vector.tensor_copy, wg_woven[:, PACK * SCALAR_SLOTS :], wg_gathered[:, :, SCALAR_SLOTS:])
        wg_q = mx_operand("wg_q", E4M3)
        quantize(wg_q, wg_woven[:])
        x_along_r = mx_operand("x_along_r", E4M3, tag="wg_woven")
        quantize(x_along_r, x_turned[:].bitcast(BF16))

        dy_woven = sb("dy_woven", PACK * K, BF16, tag="wg_gathered")
        dy_q = mx_operand("dy_q", E5M2)
        for m in range(BLOCKS):
            weave(nc.scalar.copy, woven_block(dy_woven, m), dy_raw[:, :, block(m)])
        quantize(dy_q, dy_woven[:])

        wu_windows = plane_windows("wu", "wg_then_wu")
        load_planes(wu_windows, wu, range(PACK))
        for m in range(BLOCKS):
            product(low[m], x_along_d, m, wg_q)
        scale_and_turn(low, us_col)
        silu = [sb("silu%d" % j, K, F32) for j in range(BLOCKS)]
        slope = [sb("slope%d" % j, K, F32) for j in range(BLOCKS)]
        for j in range(BLOCKS):
            nc.scalar.activation(silu[j][:], high[j][:], ACT.Silu, scale=tg_col[:, j : j + 1])
            nc.scalar.activation(slope[j][:], high[j][:], ACT.Tanh, scale=tg_neg_half[:, j : j + 1])

        wd_gathered = sb_planes("wd_gathered", BF16, tag="x_turned")
        gather_planes(wd_gathered, wd_windows, range(PACK))
        tu_gathered = sb("tu_gathered", K, F32, tag="wd0")
        tu_turned = gather_scale(tu_row, tu_gathered, low[0])
        tu_col = sb("tu_col", BLOCKS, F32)
        tg_tu = sb("tg_tu", BLOCKS, F32)
        nc.scalar.copy(out=tu_col[:], in_=tu_turned)
        nc.gpsimd.tensor_tensor(tg_tu[:], tg_col[:], tu_col[:], ALU.mult)

        wd_woven = sb("wd_woven", PACK * K, BF16)
        weave(nc.vector.tensor_copy, wd_woven[:], wd_gathered[:])
        wd_q = mx_operand("wd_q", E4M3)
        quantize(wd_q, wd_woven[:])
        for m in range(BLOCKS):
            product(low[m], dy_q, m, wd_q)
        scale_and_turn(low, wt_us)

        one_less_s = sb_planes("one_less_s", F32, tag="x_turned")
        for j in range(BLOCKS):
            nc.scalar.activation(one_less_s[:, j, :], slope[j][:], ACT.Identity, scale=0.5, bias=0.5)
            nc.vector.scalar_tensor_tensor(slope[j][:], silu[j][:], -1.0, one_less_s[:, j, :], ALU.add, ALU.mult)

        du_turned = sb("du_turned", 2 * K, F32)
        du_q = mx_operand("du_q", E5M2)
        for j in range(BLOCKS):
            nc.vector.scalar_tensor_tensor(
                rounded[j][:, 0:K], high[j][:], tu_col[:, j : j + 1], silu[j][:], ALU.mult, ALU.mult
            )
            rows_to_partitions(j, low[j], du_turned)
        for j in range(BLOCKS):
            quantize(du_q, du_turned[:, PAIRS * j : PAIRS * (j + 1)].bitcast(BF16), block(j))
        for k in range(WINDOWS_1):
            product(low[k], x_along_r, k, du_q)

        wu_gathered = sb_planes("wu_gathered", BF16, tag="wd_woven")
        gather_planes(wu_gathered, wu_windows, range(PACK))
        wu_woven = sb("wu_woven", PACK * K, BF16)
        for j in range(BLOCKS):
            weave(nc.scalar.copy, woven_block(wu_woven, j), wu_gathered[:, :, block(j)])
        wu_q = mx_operand("wu_q", E4M3)
        quantize(wu_q, wu_woven[:])
        for j in range(BLOCKS):
            nc.vector.scalar_tensor_tensor(slope[j][:], slope[j][:], 1.0, high[j][:], ALU.add, ALU.mult)

        for k in range(WINDOWS_1):
            put(low[k], silu[k][:], windows_1[k], out_1, k)

        free_first = low[WINDOWS_1:] + low[:WINDOWS_1]
        for m in range(BLOCKS):
            product(free_first[m], x_along_d, m, wu_q)
        scale_and_turn(free_first, us_col)
        for k in range(WINDOWS_1, BLOCKS):
            product(low[k], x_along_r, k, du_q)
        for j in range(BLOCKS):
            nc.vector.scalar_tensor_tensor(
                rounded[j][:, 0:K], high[j][:], tg_tu[:, j : j + 1], slope[j][:], ALU.mult, ALU.mult
            )
        put(low[2], slope[2][:], windows_1[0], out_1, 2)
        dg_turned = sb("dg_turned", 2 * K, F32)
        for j in range(BLOCKS):
            rows_to_partitions(j, high[j], dg_turned)
        dg_q = mx_operand("dg_q", E5M2, tag="slope2")
        quantize(dg_q, dg_turned[:].bitcast(BF16))
        put(low[3], rounded[3][:].bitcast(F32), windows_1[1], out_1, 3)

        for k in range(BLOCKS):
            product(high[k], x_along_r, k, dg_q)
            put(high[k], staged[k][:], windows_0[k % WINDOWS_0], out_0, k)
